import numpy as np
import ml_dtypes


def mxq(x, axis, fmt="e4m3"):
    dtype, down = {"e4m3": (ml_dtypes.float8_e4m3fn, 7), "e5m2": (ml_dtypes.float8_e5m2, 14)}[fmt]
    v = np.moveaxis(np.asarray(x, np.float32).astype(ml_dtypes.bfloat16).astype(np.float64), axis, -1)
    blocks = v.reshape(v.shape[:-1] + (-1, 32))
    amax = np.abs(blocks).max(-1, keepdims=True)
    byte = np.maximum(np.where(amax > 0, np.frexp(amax)[1] - 1 + 127, 0) - down, 1)
    scale = np.exp2(byte - 127.0)
    codes = (blocks / scale).astype(np.float32).astype(dtype).astype(np.float64)
    return np.moveaxis((codes * scale).reshape(v.shape), -1, axis)


WIDE = False


def mx_kscale(k):
    if not WIDE:
        return np.ones(k)
    levels = np.array([10, -10, 5, -5, 0])
    if k % 512:
        return np.exp2(np.random.permutation(np.resize(levels, k // 32))).repeat(32)
    a = np.empty((k // 512, 16))
    for p in range(k // 512):
        a[p, :8] = np.random.permutation(np.resize(levels, 8))
        for g in range(8):
            far = levels[np.abs(levels - a[p, g]) >= 10]
            a[p, g + 8] = far[np.random.randint(len(far))]
    return np.exp2(a.ravel()).repeat(32)


def f64(x):
    return np.asarray(x).astype(np.float64)


def striped(idx):
    return np.tile(idx.reshape(-1, 16).T, (8, 1)).astype(np.uint16)


def unstriped(offs):
    return offs[:16].T.reshape(-1).astype(np.int64)


def striped8(idx):
    return np.concatenate([x.reshape(-1, 16).T for x in idx]).astype(np.uint16)


def runs(offs, k):
    lists = np.stack([offs[16 * r : 16 * r + 16].T.reshape(-1) for r in range(8)]).astype(np.int64)
    return lists[np.arange(k) % 512 // 64]


def pack_weight(w):
    k, n = w.shape
    w = f64(np.asarray(w, np.float32).astype(ml_dtypes.bfloat16)).reshape(k // 32, 32, n)
    amax = np.abs(w).max(1)
    byte = np.clip(np.where(amax > 0, np.frexp(amax)[1] - 1 + 127 - 7, 1), 1, 254)
    scaled = (w * np.exp2(127.0 - byte)[:, None, :]).reshape(k, n).astype(np.float32)
    words = np.ascontiguousarray(scaled.reshape(k // 512, 128, 4, n).transpose(0, 1, 3, 2)).astype(ml_dtypes.float8_e4m3fn).view(np.uint8)
    return words, np.ascontiguousarray(byte.astype(np.uint8).reshape(k // 512, 16, n))


def unpack_weight(words, scales):
    g, p, n, _ = words.shape
    vals = np.ascontiguousarray(words).view(ml_dtypes.float8_e4m3fn).astype(np.float64) * np.repeat(np.exp2(scales.astype(np.float64) - 127.0), 8, axis=1)[..., None]
    return vals.transpose(0, 1, 3, 2).reshape(g * 512, n)


def sigmoid(v):
    return 1.0 / (1.0 + np.exp(-np.maximum(v, -700.0)))


K, T, S, H, G = 512, 1024, 512, 512, 2048


def setup_inputs():
    n = np.random.standard_normal
    s = mx_kscale(K)[:, None]
    packed_xT = pack_weight(n((K, T)) * s)
    packed_dT = pack_weight(n((K, G)) / s)
    return {
        "x_words": packed_xT[0],
        "x_scales": packed_xT[1],
        "w1": (n((K, H)) / np.sqrt(K) / s).astype(np.float32),
        "w2": (n((K, H)) / np.sqrt(K) / s).astype(np.float32),
        "gs": (np.random.uniform(0.5, 1.5, (K, 1)) * s).astype(np.float32),
        "d_words": packed_dT[0],
        "d_scales": packed_dT[1],
        "offs": striped(np.random.permutation(T)[:S]),
        "two": striped(np.random.permutation(T)[:S]),
        "n1": striped8(np.stack([np.random.permutation(S) for _ in range(8)])),
        "n2": striped8(np.stack([np.random.permutation(S) for _ in range(8)])),
        "k1": striped8(np.random.randint(0, G, (8, H))),
        "n3": striped8(np.stack([np.random.permutation(S) for _ in range(8)])),
        "n4": striped8(np.stack([np.random.permutation(S) for _ in range(8)])),
    }


def reference(x_words, x_scales, w1, w2, gs, d_words, d_scales, offs, two, n1, n2, k1, n3, n4):
    d_k1 = unpack_weight(d_words, d_scales)[np.arange(K)[:, None], runs(k1, K)]
    xq = unpack_weight(x_words, x_scales)[:, unstriped(offs)]
    y = mxq(f64(w1), 0, "e4m3").T @ xq
    x_two = unpack_weight(x_words, x_scales)[:, unstriped(two)]
    d = mxq(f64(w2), 0, "e4m3").T @ x_two
    z = f64(gs) * (y + (sigmoid(d[np.arange(H)[:, None], runs(n2, H)] - d)) * (y[np.arange(H)[:, None], runs(n1, H)] - y))
    h = 0.0625 * ((d_k1.T @ mxq(z, 0, "e4m3")))
    return (h[np.arange(H)[:, None], runs(n3, H)]) * (h[np.arange(H)[:, None], runs(n4, H)])

@@ -1,0 +1,238 @@
+from contextlib import ExitStack
+
+import concourse.mybir as mybir
+
+K, T, S, H, G = 512, 1024, 512, 512, 2048
+FLOPS = 3 * 2 * K * H * S
+
+F32 = mybir.dt.float32
+BF16 = mybir.dt.bfloat16
+I32 = mybir.dt.int32
+U32 = mybir.dt.uint32
+U16 = mybir.dt.uint16
+U8 = mybir.dt.uint8
+FP8X4 = mybir.dt.float8_e4m3fn_x4
+ALU = mybir.AluOpType
+ACT = mybir.ActivationFunctionType
+
+P = 128
+PACK = 4
+GROUP = 16
+HALF = S // 2
+Z_CHUNKS = ((0, 256), (256, 384), (384, 512))
+LAST_PIECES = ((0, 256), (256, 384), (384, 512))
+
+
+def tile_picked_twqpullbprod_none_p_kernel(
+    tc, x_words, x_scales, w1, w2, gs, d_words, d_scales, offs, two, n1, n2, k1, n3, n4, out
+):
+    nc = tc.nc
+    with ExitStack() as ctx:
+        keep = ctx.enter_context(tc.tile_pool(name="keep", bufs=1))
+        psum = ctx.enter_context(tc.psum_pool(name="psum", bufs=8))
+
+        def sb(name, shape, dtype):
+            return keep.tile(shape, dtype, name=name, align_bytes=64)
+
+        def load_list(name, src):
+            lst = keep.tile([P, S // GROUP], U16, name=name)
+            nc.sync.dma_start(lst[:], src)
+            return lst
+
+        def entries(lst, lo, hi):
+            return lst[:, lo // GROUP : hi // GROUP]
+
+        x_scale_tab = sb("x_scale_tab", [P, T], U8)
+        d_scale_tab = sb("d_scale_tab", [P, G], U8)
+        code_scales = sb("code_scales", [P, H], U8)
+        warm = sb("warm", [P, 8], F32)
+        nc.vector.memset(x_scale_tab[:].bitcast(I32), 0)
+        nc.vector.memset(warm[:], 0.0)
+        nc.vector.memset(d_scale_tab[:].bitcast(I32), 0)
+        nc.vector.memset(code_scales[:].bitcast(I32), 0)
+
+        x_word_tab = sb("x_word_tab", [P, T], U32)
+        nc.sync.dma_start(x_word_tab[:].bitcast(I32), x_words[0].rearrange("p n t -> p (n t)").bitcast(I32))
+        for q in range(4):
+            nc.sync.dma_start(
+                x_scale_tab[32 * q : 32 * q + 4, :].bitcast(I32), x_scales[0, 4 * q : 4 * q + 4, :].bitcast(I32)
+            )
+        two_l = load_list("two_l", two)
+        warm_out = sb("warm_out", [P, 8], F32)
+        nc.scalar.activation(warm_out[:], warm[:], ACT.Sigmoid)
+        offs_l = load_list("offs_l", offs)
+
+        def load_weight(name, w):
+            halves = []
+            for u in range(2):
+                raw = sb(f"{name}_raw{u}", [P, PACK, HALF], F32)
+                nc.sync.dma_start(raw[:], w.rearrange("(p j) c -> p j c", j=PACK)[:, :, u * HALF : (u + 1) * HALF])
+                halves.append(raw)
+            return halves
+
+        w2_raw = load_weight("w2", w2)
+        nc.sync.dma_start(d_scale_tab[0:P:8, :].bitcast(I32), d_scales[0].bitcast(I32))
+        k1_l = load_list("k1_l", k1)
+        w1_raw = load_weight("w1", w1)
+        d_word_tab = sb("d_word_tab", [P, G], U32)
+        nc.sync.dma_start(d_word_tab[:].bitcast(I32), d_words[0].rearrange("p n t -> p (n t)").bitcast(I32))
+        n2_l = load_list("n2_l", n2)
+        gs_t = sb("gs_t", [P, PACK], F32)
+        nc.sync.dma_start(gs_t[:], gs.rearrange("(p t) o -> p (t o)", t=PACK))
+        n1_l = load_list("n1_l", n1)
+        n3_l = load_list("n3_l", n3)
+        n4_l = load_list("n4_l", n4)
+
+        def pick(name, table, lst, dtype):
+            picked = sb(name, [P, S], dtype)
+            nc.vector.tensor_copy(picked[:], table[:].indirect(lst[:]))
+            return picked
+
+        x2_words = pick("x2_words", x_word_tab, two_l, U32)
+        x2_scales = pick("x2_scales", x_scale_tab, two_l, U8)
+        x1_words = pick("x1_words", x_word_tab, offs_l, U32)
+        x1_scales = pick("x1_scales", x_scale_tab, offs_l, U8)
+
+        def round_weight(name, halves):
+            grouped = sb(f"{name}_grouped", [P, PACK * H], BF16)
+            view = grouped[:].rearrange("p (t m j) -> p m t j", t=PACK, j=PACK)
+            m_half = HALF // PACK
+            for u in range(2):
+                nc.scalar.copy(
+                    view[:, u * m_half : (u + 1) * m_half, :, :],
+                    halves[u][:].rearrange("p j (m t) -> p m t j", t=PACK),
+                )
+            return grouped
+
+        def quantise(name, grouped, width):
+            codes = sb(f"{name}_codes", [P, width], U32)
+            scales = sb(f"{name}_scales", [P, width], U8)
+            nc.vector.quantize_mx(out=codes[:].bitcast(FP8X4), scales=scales[:], in_=grouped)
+            return codes, scales
+
+        def product(name, stat, t, moving, width):
+            acc = psum.tile([P, width], F32, name=name, tag="bank")
+            cols = slice(t * P, (t + 1) * P)
+            nc.tensor.matmul_mx(
+                out=acc[:],
+                lhsT=stat[0][:, cols].bitcast(FP8X4),
+                lhsT_scale=stat[1][:, cols],
+                rhs=moving[0][:].bitcast(FP8X4),
+                rhs_scale=moving[1][:],
+                start=True,
+                stop=True,
+            )
+            return acc
+
+        w2_grouped = round_weight("w2", w2_raw)
+
+        picked_scales = pick("picked_scales", d_scale_tab, k1_l, U8)
+        dealt_scales = sb("dealt_scales", [P, H], U8)
+        nc.vector.tensor_copy(
+            dealt_scales[:].rearrange("p (t m) -> p t m", t=PACK), picked_scales[:].rearrange("p (m t) -> p t m", t=PACK)
+        )
+        for r in range(4):
+            nc.sync.dma_start(code_scales[r:P:32, :].bitcast(I32), dealt_scales[8 * r : P : 32, :].bitcast(I32))
+
+        w2_q = quantise("w2", w2_grouped[:], H)
+        d_win, d_own = [], []
+        for t in range(PACK):
+            acc = product(f"d_acc{t}", w2_q, t, (x2_words, x2_scales), S)
+            win = sb(f"d_win{t}", [P, S], F32)
+            own = sb(f"d_own{t}", [P, S], F32)
+            nc.scalar.copy(win[:], acc[:])
+            nc.scalar.copy(own[:], acc[:])
+            d_win.append(win)
+            d_own.append(own)
+
+        w1_grouped = round_weight("w1", w1_raw)
+        w1_q = quantise("w1", w1_grouped[:], H)
+
+        picked_words = pick("picked_words", d_word_tab, k1_l, U32)
+        code_words = sb("code_words", [P, H], U32)
+        nc.vector.tensor_copy(
+            code_words[:].rearrange("p (t c i) -> p c t i", t=PACK, i=4),
+            picked_words[:].rearrange("p (c i t) -> p c t i", t=PACK, i=4),
+        )
+
+        diffs = []
+        for t in range(PACK):
+            diff = sb(f"diff{t}", [P, S], F32)
+            for lo in (0, HALF):
+                nc.vector.tensor_tensor(
+                    diff[:, lo : lo + HALF],
+                    d_win[t][:].indirect(entries(n2_l, lo, lo + HALF)),
+                    d_own[t][:, lo : lo + HALF],
+                    ALU.subtract,
+                )
+            diffs.append(diff)
+
+        y_own = sb("y_own", [P, PACK, S], F32)
+        step = sb("step", [P, PACK, S], F32)
+        pulls, gates = [], []
+
+        def gated(t):
+            nc.vector.tensor_tensor(step[:, t, :], gates[t][:], pulls[t][:], ALU.mult)
+
+        for t in range(PACK):
+            acc = product(f"y_acc{t}", w1_q, t, (x1_words, x1_scales), S)
+            win = sb(f"y_win{t}", [P, S], F32)
+            nc.scalar.activation(win[:], acc[:], ACT.Copy, scale=gs_t[:, t : t + 1])
+            nc.scalar.activation(y_own[:, t, :], acc[:], ACT.Copy, scale=gs_t[:, t : t + 1])
+            pull = sb(f"pull{t}", [P, S], F32)
+            for lo in (0, HALF):
+                nc.vector.tensor_tensor(
+                    pull[:, lo : lo + HALF],
+                    win[:].indirect(entries(n1_l, lo, lo + HALF)),
+                    y_own[:, t, lo : lo + HALF],
+                    ALU.subtract,
+                )
+            gate = sb(f"gate{t}", [P, S], F32)
+            nc.scalar.activation(gate[:], diffs[t][:], ACT.Sigmoid)
+            pulls.append(pull)
+            gates.append(gate)
+            if t > 0:
+                gated(t - 1)
+        gated(PACK - 1)
+
+        h_win = [sb(f"h_win{t}", [P, S], F32) for t in range(PACK)]
+        z_grouped = []
+
+        def blend(c):
+            lo, hi = Z_CHUNKS[c]
+            grouped = sb(f"z_grouped{c}", [P, PACK * (hi - lo)], BF16)
+            nc.vector.tensor_tensor(
+                grouped[:].rearrange("p (c i t) -> p c t i", t=PACK, i=4),
+                step[:, :, lo:hi].rearrange("p t (c i) -> p c t i", i=4),
+                y_own[:, :, lo:hi].rearrange("p t (c i) -> p c t i", i=4),
+                ALU.add,
+            )
+            z_grouped.append(grouped)
+
+        def coded_layer(c):
+            lo, hi = Z_CHUNKS[c]
+            z_q = quantise(f"z{c}", z_grouped[c][:], hi - lo)
+            for t in range(PACK):
+                acc = product(f"h_acc{c}_{t}", (code_words, code_scales), t, z_q, hi - lo)
+                nc.scalar.activation(h_win[t][:, lo:hi], acc[:], ACT.Copy, scale=0.0625)
+
+        blend(0)
+        for c in range(1, len(Z_CHUNKS)):
+            blend(c)
+            coded_layer(c - 1)
+        coded_layer(len(Z_CHUNKS) - 1)
+
+        out_rows = out.rearrange("(p t) n -> p t n", t=PACK)
+        for t in range(PACK):
+            last = t == PACK - 1
+            pieces = LAST_PIECES if last else ((0, HALF), (HALF, S))
+            first = sb(f"first{t}", [P, S], F32)
+            res = sb(f"res{t}", [P, S], F32)
+            for lo, hi in ((0, HALF), (HALF, S)):
+                nc.vector.tensor_copy(first[:, lo:hi], h_win[t][:].indirect(entries(n3_l, lo, hi)))
+            for lo, hi in pieces:
+                nc.vector.tensor_tensor(res[:, lo:hi], h_win[t][:].indirect(entries(n4_l, lo, hi)), first[:, lo:hi], ALU.mult)
+                if last:
+                    nc.sync.dma_start(out_rows[:, t, lo:hi], res[:, lo:hi])
+            if not last:
+                nc.sync.dma_start(out_rows[:, t, :], res[:])

@@ -46,21 +46,21 @@ def tile_picked_twqpullbprod_none_p_kernel(
         d_scale_tab = sb("d_scale_tab", [P, G], U8)
         code_scales = sb("code_scales", [P, H], U8)
         warm = sb("warm", [P, 8], F32)
-        nc.vector.memset(x_scale_tab[:].bitcast(I32), 0)
+        nc.gpsimd.memset(x_scale_tab[:].bitcast(I32), 0)
         nc.vector.memset(warm[:], 0.0)
         nc.vector.memset(d_scale_tab[:].bitcast(I32), 0)
         nc.vector.memset(code_scales[:].bitcast(I32), 0)
 
-        x_word_tab = sb("x_word_tab", [P, T], U32)
-        nc.sync.dma_start(x_word_tab[:].bitcast(I32), x_words[0].rearrange("p n t -> p (n t)").bitcast(I32))
+        two_l = load_list("two_l", two)
+        offs_l = load_list("offs_l", offs)
         for q in range(4):
             nc.sync.dma_start(
                 x_scale_tab[32 * q : 32 * q + 4, :].bitcast(I32), x_scales[0, 4 * q : 4 * q + 4, :].bitcast(I32)
             )
-        two_l = load_list("two_l", two)
+        x_word_tab = sb("x_word_tab", [P, T], U32)
+        nc.sync.dma_start(x_word_tab[:].bitcast(I32), x_words[0].rearrange("p n t -> p (n t)").bitcast(I32))
         warm_out = sb("warm_out", [P, 8], F32)
         nc.scalar.activation(warm_out[:], warm[:], ACT.Sigmoid)
-        offs_l = load_list("offs_l", offs)
 
         def load_weight(name, w):
             halves = []
@@ -71,9 +71,9 @@ def tile_picked_twqpullbprod_none_p_kernel(
             return halves
 
         w2_raw = load_weight("w2", w2)
+        w1_raw = load_weight("w1", w1)
         nc.sync.dma_start(d_scale_tab[0:P:8, :].bitcast(I32), d_scales[0].bitcast(I32))
         k1_l = load_list("k1_l", k1)
-        w1_raw = load_weight("w1", w1)
         d_word_tab = sb("d_word_tab", [P, G], U32)
         nc.sync.dma_start(d_word_tab[:].bitcast(I32), d_words[0].rearrange("p n t -> p (n t)").bitcast(I32))
         n2_l = load_list("n2_l", n2)
@@ -88,10 +88,10 @@ def tile_picked_twqpullbprod_none_p_kernel(
             nc.vector.tensor_copy(picked[:], table[:].indirect(lst[:]))
             return picked
 
-        x2_words = pick("x2_words", x_word_tab, two_l, U32)
         x2_scales = pick("x2_scales", x_scale_tab, two_l, U8)
-        x1_words = pick("x1_words", x_word_tab, offs_l, U32)
         x1_scales = pick("x1_scales", x_scale_tab, offs_l, U8)
+        x2_words = pick("x2_words", x_word_tab, two_l, U32)
+        x1_words = pick("x1_words", x_word_tab, offs_l, U32)
 
         def round_weight(name, halves):
             grouped = sb(f"{name}_grouped", [P, PACK * H], BF16)
@@ -125,77 +125,63 @@ def tile_picked_twqpullbprod_none_p_kernel(
             return acc
 
         w2_grouped = round_weight("w2", w2_raw)
+        w1_grouped = round_weight("w1", w1_raw)
+        w2_q = quantise("w2", w2_grouped[:], H)
 
         picked_scales = pick("picked_scales", d_scale_tab, k1_l, U8)
+        picked_words = pick("picked_words", d_word_tab, k1_l, U32)
         dealt_scales = sb("dealt_scales", [P, H], U8)
         nc.vector.tensor_copy(
             dealt_scales[:].rearrange("p (t m) -> p t m", t=PACK), picked_scales[:].rearrange("p (m t) -> p t m", t=PACK)
         )
         for r in range(4):
             nc.sync.dma_start(code_scales[r:P:32, :].bitcast(I32), dealt_scales[8 * r : P : 32, :].bitcast(I32))
-
-        w2_q = quantise("w2", w2_grouped[:], H)
-        d_win, d_own = [], []
-        for t in range(PACK):
-            acc = product(f"d_acc{t}", w2_q, t, (x2_words, x2_scales), S)
-            win = sb(f"d_win{t}", [P, S], F32)
-            own = sb(f"d_own{t}", [P, S], F32)
-            nc.scalar.copy(win[:], acc[:])
-            nc.scalar.copy(own[:], acc[:])
-            d_win.append(win)
-            d_own.append(own)
-
-        w1_grouped = round_weight("w1", w1_raw)
         w1_q = quantise("w1", w1_grouped[:], H)
-
-        picked_words = pick("picked_words", d_word_tab, k1_l, U32)
         code_words = sb("code_words", [P, H], U32)
         nc.vector.tensor_copy(
             code_words[:].rearrange("p (t c i) -> p c t i", t=PACK, i=4),
             picked_words[:].rearrange("p (c i t) -> p c t i", t=PACK, i=4),
         )
 
+        windows = [sb(f"window{t}", [P, 2 * S], F32) for t in range(PACK)]
+        for t in range(PACK):
+            acc = product(f"d_acc{t}", w2_q, t, (x2_words, x2_scales), S)
+            places = [windows[t][:, :S], windows[t ^ 1][:, S:]]
+            for place in places if t % 2 == 0 else reversed(places):
+                nc.scalar.copy(place, acc[:])
+
         diffs = []
         for t in range(PACK):
             diff = sb(f"diff{t}", [P, S], F32)
-            for lo in (0, HALF):
-                nc.vector.tensor_tensor(
-                    diff[:, lo : lo + HALF],
-                    d_win[t][:].indirect(entries(n2_l, lo, lo + HALF)),
-                    d_own[t][:, lo : lo + HALF],
-                    ALU.subtract,
-                )
+            nc.vector.tensor_tensor(diff[:], windows[t][:].indirect(n2_l[:]), windows[t ^ 1][:, S:], ALU.subtract)
             diffs.append(diff)
 
         y_own = sb("y_own", [P, PACK, S], F32)
         step = sb("step", [P, PACK, S], F32)
         pulls, gates = [], []
 
-        def gated(t):
-            nc.vector.tensor_tensor(step[:, t, :], gates[t][:], pulls[t][:], ALU.mult)
+        def make_gate(t):
+            gate = sb(f"gate{t}", [P, S], F32)
+            nc.scalar.activation(gate[:], diffs[t][:], ACT.Sigmoid)
+            gates.append(gate)
+
+        def gated(t, lo, hi):
+            nc.vector.tensor_tensor(step[:, t, lo:hi], gates[t][:, lo:hi], pulls[t][:, lo:hi], ALU.mult)
 
         for t in range(PACK):
             acc = product(f"y_acc{t}", w1_q, t, (x1_words, x1_scales), S)
-            win = sb(f"y_win{t}", [P, S], F32)
-            nc.scalar.activation(win[:], acc[:], ACT.Copy, scale=gs_t[:, t : t + 1])
+            nc.scalar.activation(windows[t][:, :S], acc[:], ACT.Copy, scale=gs_t[:, t : t + 1])
             nc.scalar.activation(y_own[:, t, :], acc[:], ACT.Copy, scale=gs_t[:, t : t + 1])
             pull = sb(f"pull{t}", [P, S], F32)
-            for lo in (0, HALF):
-                nc.vector.tensor_tensor(
-                    pull[:, lo : lo + HALF],
-                    win[:].indirect(entries(n1_l, lo, lo + HALF)),
-                    y_own[:, t, lo : lo + HALF],
-                    ALU.subtract,
-                )
-            gate = sb(f"gate{t}", [P, S], F32)
-            nc.scalar.activation(gate[:], diffs[t][:], ACT.Sigmoid)
+            nc.vector.tensor_tensor(pull[:], windows[t][:].indirect(n1_l[:]), y_own[:, t, :], ALU.subtract)
             pulls.append(pull)
-            gates.append(gate)
             if t > 0:
-                gated(t - 1)
-        gated(PACK - 1)
+                make_gate(t - 1)
+                gated(t - 1, 0, S)
+        make_gate(PACK - 1)
+        gated(PACK - 1, 0, HALF)
+        gated(PACK - 1, HALF, S)
 
-        h_win = [sb(f"h_win{t}", [P, S], F32) for t in range(PACK)]
         z_grouped = []
 
         def blend(c):
@@ -209,30 +195,42 @@ def tile_picked_twqpullbprod_none_p_kernel(
             )
             z_grouped.append(grouped)
 
-        def coded_layer(c):
+        z_q = []
+
+        def quantise_z(c):
             lo, hi = Z_CHUNKS[c]
-            z_q = quantise(f"z{c}", z_grouped[c][:], hi - lo)
-            for t in range(PACK):
-                acc = product(f"h_acc{c}_{t}", (code_words, code_scales), t, z_q, hi - lo)
-                nc.scalar.activation(h_win[t][:, lo:hi], acc[:], ACT.Copy, scale=0.0625)
+            z_q.append(quantise(f"z{c}", z_grouped[c][:], hi - lo))
+
+        def coded_layer(c, t):
+            lo, hi = Z_CHUNKS[c]
+            acc = product(f"h_acc{c}_{t}", (code_words, code_scales), t, z_q[c], hi - lo)
+            nc.scalar.activation(windows[t][:, lo:hi], acc[:], ACT.Copy, scale=0.0625)
 
         blend(0)
         for c in range(1, len(Z_CHUNKS)):
             blend(c)
-            coded_layer(c - 1)
-        coded_layer(len(Z_CHUNKS) - 1)
+            quantise_z(c - 1)
+        quantise_z(len(Z_CHUNKS) - 1)
+        for t in range(PACK):
+            for c in range(len(Z_CHUNKS)):
+                coded_layer(c, t)
 
         out_rows = out.rearrange("(p t) n -> p t n", t=PACK)
-        for t in range(PACK):
-            last = t == PACK - 1
-            pieces = LAST_PIECES if last else ((0, HALF), (HALF, S))
+        firsts = []
+
+        def fetch(t):
             first = sb(f"first{t}", [P, S], F32)
+            nc.vector.tensor_copy(first[:], windows[t][:].indirect(n3_l[:]))
+            firsts.append(first)
+
+        def finish(t, pieces):
             res = sb(f"res{t}", [P, S], F32)
-            for lo, hi in ((0, HALF), (HALF, S)):
-                nc.vector.tensor_copy(first[:, lo:hi], h_win[t][:].indirect(entries(n3_l, lo, hi)))
             for lo, hi in pieces:
-                nc.vector.tensor_tensor(res[:, lo:hi], h_win[t][:].indirect(entries(n4_l, lo, hi)), first[:, lo:hi], ALU.mult)
-                if last:
-                    nc.sync.dma_start(out_rows[:, t, lo:hi], res[:, lo:hi])
-            if not last:
-                nc.sync.dma_start(out_rows[:, t, :], res[:])
+                nc.vector.tensor_tensor(res[:, lo:hi], windows[t][:].indirect(entries(n4_l, lo, hi)), firsts[t][:, lo:hi], ALU.mult)
+                nc.sync.dma_start(out_rows[:, t, lo:hi], res[:, lo:hi])
+
+        fetch(0)
+        for t in range(1, PACK):
+            fetch(t)
+            finish(t - 1, ((0, S),))
+        finish(PACK - 1, LAST_PIECES)

@@ -50,33 +50,35 @@ def tile_picked_twqpullbprod_none_p_kernel(
         nc.vector.memset(warm[:], 0.0)
         nc.vector.memset(d_scale_tab[:].bitcast(I32), 0)
         nc.vector.memset(code_scales[:].bitcast(I32), 0)
+        windows = [sb(f"window{t}", [P, 2 * S], F32) for t in range(PACK)]
+        for t in range(PACK):
+            nc.vector.memset(windows[t][:, S:].bitcast(I32), 0)
+
+        def load_weight(name, w, lo, hi):
+            raw = sb(f"{name}_raw{lo}", [P, PACK, hi - lo], F32)
+            nc.sync.dma_start(raw[:], w.rearrange("(p j) c -> p j c", j=PACK)[:, :, lo:hi])
+            return raw, lo, hi
 
         two_l = load_list("two_l", two)
-        offs_l = load_list("offs_l", offs)
         for q in range(4):
             nc.sync.dma_start(
                 x_scale_tab[32 * q : 32 * q + 4, :].bitcast(I32), x_scales[0, 4 * q : 4 * q + 4, :].bitcast(I32)
             )
-        x_word_tab = sb("x_word_tab", [P, T], U32)
-        nc.sync.dma_start(x_word_tab[:].bitcast(I32), x_words[0].rearrange("p n t -> p (n t)").bitcast(I32))
         warm_out = sb("warm_out", [P, 8], F32)
         nc.scalar.activation(warm_out[:], warm[:], ACT.Sigmoid)
-
-        def load_weight(name, w):
-            halves = []
-            for u in range(2):
-                raw = sb(f"{name}_raw{u}", [P, PACK, HALF], F32)
-                nc.sync.dma_start(raw[:], w.rearrange("(p j) c -> p j c", j=PACK)[:, :, u * HALF : (u + 1) * HALF])
-                halves.append(raw)
-            return halves
-
-        w2_raw = load_weight("w2", w2)
-        w1_raw = load_weight("w1", w1)
-        nc.sync.dma_start(d_scale_tab[0:P:8, :].bitcast(I32), d_scales[0].bitcast(I32))
+        w2_raw = [load_weight("w2", w2, 0, 256)]
         k1_l = load_list("k1_l", k1)
+        nc.sync.dma_start(d_scale_tab[0:P:8, :].bitcast(I32), d_scales[0].bitcast(I32))
+        x_word_tab = sb("x_word_tab", [P, T], U32)
+        nc.sync.dma_start(x_word_tab[:].bitcast(I32), x_words[0].rearrange("p n t -> p (n t)").bitcast(I32))
+        w2_raw.append(load_weight("w2", w2, 256, 384))
+        w2_raw.append(load_weight("w2", w2, 384, 512))
+        w1_raw = [load_weight("w1", w1, 0, 256)]
+        offs_l = load_list("offs_l", offs)
+        n2_l = load_list("n2_l", n2)
+        w1_raw.append(load_weight("w1", w1, 256, 512))
         d_word_tab = sb("d_word_tab", [P, G], U32)
         nc.sync.dma_start(d_word_tab[:].bitcast(I32), d_words[0].rearrange("p n t -> p (n t)").bitcast(I32))
-        n2_l = load_list("n2_l", n2)
         gs_t = sb("gs_t", [P, PACK], F32)
         nc.sync.dma_start(gs_t[:], gs.rearrange("(p t) o -> p (t o)", t=PACK))
         n1_l = load_list("n1_l", n1)
@@ -89,20 +91,20 @@ def tile_picked_twqpullbprod_none_p_kernel(
             return picked
 
         x2_scales = pick("x2_scales", x_scale_tab, two_l, U8)
-        x1_scales = pick("x1_scales", x_scale_tab, offs_l, U8)
+        picked_scales = pick("picked_scales", d_scale_tab, k1_l, U8)
         x2_words = pick("x2_words", x_word_tab, two_l, U32)
-        x1_words = pick("x1_words", x_word_tab, offs_l, U32)
 
-        def round_weight(name, halves):
-            grouped = sb(f"{name}_grouped", [P, PACK * H], BF16)
+        def round_weight(grouped, piece):
+            raw, lo, hi = piece
             view = grouped[:].rearrange("p (t m j) -> p m t j", t=PACK, j=PACK)
-            m_half = HALF // PACK
-            for u in range(2):
-                nc.scalar.copy(
-                    view[:, u * m_half : (u + 1) * m_half, :, :],
-                    halves[u][:].rearrange("p j (m t) -> p m t j", t=PACK),
+            nc.scalar.copy(view[:, lo // PACK : hi // PACK, :, :], raw[:].rearrange("p j (m t) -> p m t j", t=PACK))
+
+        def deal(dealt, picked, q):
+            for t in range(PACK):
+                nc.sync.dma_start(
+                    dealt[:].bitcast(I32).rearrange("p (t g q) -> p t g q", t=PACK, q=q)[:, t],
+                    picked[:].bitcast(I32).rearrange("p (g t q) -> p t g q", t=PACK, q=q)[:, t],
                 )
-            return grouped
 
         def quantise(name, grouped, width):
             codes = sb(f"{name}_codes", [P, width], U32)
@@ -124,37 +126,39 @@ def tile_picked_twqpullbprod_none_p_kernel(
             )
             return acc
 
-        w2_grouped = round_weight("w2", w2_raw)
-        w1_grouped = round_weight("w1", w1_raw)
+        w2_grouped = sb("w2_grouped", [P, PACK * H], BF16)
+        w1_grouped = sb("w1_grouped", [P, PACK * H], BF16)
+        for piece in w2_raw:
+            round_weight(w2_grouped, piece)
         w2_q = quantise("w2", w2_grouped[:], H)
-
-        picked_scales = pick("picked_scales", d_scale_tab, k1_l, U8)
-        picked_words = pick("picked_words", d_word_tab, k1_l, U32)
-        dealt_scales = sb("dealt_scales", [P, H], U8)
-        nc.vector.tensor_copy(
-            dealt_scales[:].rearrange("p (t m) -> p t m", t=PACK), picked_scales[:].rearrange("p (m t) -> p t m", t=PACK)
-        )
-        for r in range(4):
-            nc.sync.dma_start(code_scales[r:P:32, :].bitcast(I32), dealt_scales[8 * r : P : 32, :].bitcast(I32))
-        w1_q = quantise("w1", w1_grouped[:], H)
-        code_words = sb("code_words", [P, H], U32)
-        nc.vector.tensor_copy(
-            code_words[:].rearrange("p (t c i) -> p c t i", t=PACK, i=4),
-            picked_words[:].rearrange("p (c i t) -> p c t i", t=PACK, i=4),
-        )
-
-        windows = [sb(f"window{t}", [P, 2 * S], F32) for t in range(PACK)]
-        for t in range(PACK):
-            acc = product(f"d_acc{t}", w2_q, t, (x2_words, x2_scales), S)
-            places = [windows[t][:, :S], windows[t ^ 1][:, S:]]
-            for place in places if t % 2 == 0 else reversed(places):
-                nc.scalar.copy(place, acc[:])
+        x1_scales = pick("x1_scales", x_scale_tab, offs_l, U8)
+        x1_words = pick("x1_words", x_word_tab, offs_l, U32)
+        round_weight(w1_grouped, w1_raw[0])
 
         diffs = []
-        for t in range(PACK):
+
+        def differences(t):
+            acc = product(f"d_acc{t}", w2_q, t, (x2_words, x2_scales), S)
+            own = sb(f"d_own{t}", [P, S], F32)
+            nc.scalar.copy(windows[t][:, :S], acc[:])
+            nc.scalar.copy(own[:], acc[:])
             diff = sb(f"diff{t}", [P, S], F32)
-            nc.vector.tensor_tensor(diff[:], windows[t][:].indirect(n2_l[:]), windows[t ^ 1][:, S:], ALU.subtract)
+            nc.vector.tensor_tensor(diff[:], windows[t][:].indirect(n2_l[:]), own[:], ALU.subtract)
             diffs.append(diff)
+
+        differences(0)
+        differences(1)
+        round_weight(w1_grouped, w1_raw[1])
+        w1_q = quantise("w1", w1_grouped[:], H)
+        picked_words = pick("picked_words", d_word_tab, k1_l, U32)
+        code_words = sb("code_words", [P, H], U32)
+        deal(code_words, picked_words, GROUP)
+        dealt_scales = keep.tile([P, H], U8, name="dealt_scales", tag="w1_raw256", align_bytes=64)
+        deal(dealt_scales, picked_scales, GROUP // 4)
+        for r in range(4):
+            nc.sync.dma_start(code_scales[r:P:32, :].bitcast(I32), dealt_scales[8 * r : P : 32, :].bitcast(I32))
+        differences(2)
+        differences(3)
 
         y_own = sb("y_own", [P, PACK, S], F32)
         step = sb("step", [P, PACK, S], F32)
@@ -215,7 +219,7 @@ def tile_picked_twqpullbprod_none_p_kernel(
             for c in range(len(Z_CHUNKS)):
                 coded_layer(c, t)
 
-        out_rows = out.rearrange("(p t) n -> p t n", t=PACK)
+        out_rows = out.rearrange("(g t q) n -> t g q n", t=PACK, q=GROUP)
         firsts = []
 
         def fetch(t):
@@ -227,7 +231,7 @@ def tile_picked_twqpullbprod_none_p_kernel(
             res = sb(f"res{t}", [P, S], F32)
             for lo, hi in pieces:
                 nc.vector.tensor_tensor(res[:, lo:hi], windows[t][:].indirect(entries(n4_l, lo, hi)), firsts[t][:, lo:hi], ALU.mult)
-                nc.sync.dma_start(out_rows[:, t, lo:hi], res[:, lo:hi])
+                nc.sync.dma_start(out_rows[t][:, :, lo:hi], res[:, lo:hi])
 
         fetch(0)
         for t in range(1, PACK):

@@ -18,6 +18,7 @@ ACT = mybir.ActivationFunctionType
 P = 128
 PACK = 4
 GROUP = 16
+RUN = 8
 HALF = S // 2
 Z_CHUNKS = ((0, 256), (256, 384), (384, 512))
 LAST_PIECES = ((0, 256), (256, 384), (384, 512))
@@ -45,14 +46,13 @@ def tile_picked_twqpullbprod_none_p_kernel(
         x_scale_tab = sb("x_scale_tab", [P, T], U8)
         d_scale_tab = sb("d_scale_tab", [P, G], U8)
         code_scales = sb("code_scales", [P, H], U8)
-        warm = sb("warm", [P, 8], F32)
         nc.gpsimd.memset(x_scale_tab[:].bitcast(I32), 0)
-        nc.vector.memset(warm[:], 0.0)
-        nc.vector.memset(d_scale_tab[:].bitcast(I32), 0)
-        nc.vector.memset(code_scales[:].bitcast(I32), 0)
         windows = [sb(f"window{t}", [P, 2 * S], F32) for t in range(PACK)]
-        for t in range(PACK):
-            nc.vector.memset(windows[t][:, S:].bitcast(I32), 0)
+        nc.vector.memset(d_scale_tab[:].bitcast(I32), 0)
+        for t in range(0, PACK, 2):
+            nc.vector.memset(windows[t][:, S:], 0.0)
+            nc.scalar.activation(windows[t + 1][:, S:], windows[t][:, S:], ACT.Sigmoid)
+        nc.vector.memset(code_scales[:].bitcast(I32), 0)
 
         def load_weight(name, w, lo, hi):
             raw = sb(f"{name}_raw{lo}", [P, PACK, hi - lo], F32)
@@ -60,19 +60,16 @@ def tile_picked_twqpullbprod_none_p_kernel(
             return raw, lo, hi
 
         two_l = load_list("two_l", two)
+        k1_l = load_list("k1_l", k1)
         for q in range(4):
             nc.sync.dma_start(
                 x_scale_tab[32 * q : 32 * q + 4, :].bitcast(I32), x_scales[0, 4 * q : 4 * q + 4, :].bitcast(I32)
             )
-        warm_out = sb("warm_out", [P, 8], F32)
-        nc.scalar.activation(warm_out[:], warm[:], ACT.Sigmoid)
-        w2_raw = [load_weight("w2", w2, 0, 256)]
-        k1_l = load_list("k1_l", k1)
         nc.sync.dma_start(d_scale_tab[0:P:8, :].bitcast(I32), d_scales[0].bitcast(I32))
+        w2_raw = [load_weight("w2", w2, 0, 256)]
         x_word_tab = sb("x_word_tab", [P, T], U32)
         nc.sync.dma_start(x_word_tab[:].bitcast(I32), x_words[0].rearrange("p n t -> p (n t)").bitcast(I32))
-        w2_raw.append(load_weight("w2", w2, 256, 384))
-        w2_raw.append(load_weight("w2", w2, 384, 512))
+        w2_raw.append(load_weight("w2", w2, 256, 512))
         w1_raw = [load_weight("w1", w1, 0, 256)]
         offs_l = load_list("offs_l", offs)
         n2_l = load_list("n2_l", n2)
@@ -94,17 +91,19 @@ def tile_picked_twqpullbprod_none_p_kernel(
         picked_scales = pick("picked_scales", d_scale_tab, k1_l, U8)
         x2_words = pick("x2_words", x_word_tab, two_l, U32)
 
-        def round_weight(grouped, piece):
+        def round_weight(grouped, piece, on_vector=0):
             raw, lo, hi = piece
-            view = grouped[:].rearrange("p (t m j) -> p m t j", t=PACK, j=PACK)
-            nc.scalar.copy(view[:, lo // PACK : hi // PACK, :, :], raw[:].rearrange("p j (m t) -> p m t j", t=PACK))
+            dst = grouped[:].rearrange("p (t m j) -> p m t j", t=PACK, j=PACK)[:, lo // PACK : hi // PACK, :, :]
+            src = raw[:].rearrange("p j (m t) -> p m t j", t=PACK)
+            if on_vector:
+                nc.vector.tensor_copy(dst[:, :on_vector], src[:, :on_vector])
+            nc.scalar.copy(dst[:, on_vector:], src[:, on_vector:])
 
-        def deal(dealt, picked, q):
-            for t in range(PACK):
-                nc.sync.dma_start(
-                    dealt[:].bitcast(I32).rearrange("p (t g q) -> p t g q", t=PACK, q=q)[:, t],
-                    picked[:].bitcast(I32).rearrange("p (g t q) -> p t g q", t=PACK, q=q)[:, t],
-                )
+        def dealt_views(dealt, picked, run):
+            return (
+                dealt[:].bitcast(I32).rearrange("p (t g r) -> p t g r", t=PACK, r=run),
+                picked[:].bitcast(I32).rearrange("p (g t r) -> p t g r", t=PACK, r=run),
+            )
 
         def quantise(name, grouped, width):
             codes = sb(f"{name}_codes", [P, width], U32)
@@ -128,8 +127,8 @@ def tile_picked_twqpullbprod_none_p_kernel(
 
         w2_grouped = sb("w2_grouped", [P, PACK * H], BF16)
         w1_grouped = sb("w1_grouped", [P, PACK * H], BF16)
-        for piece in w2_raw:
-            round_weight(w2_grouped, piece)
+        round_weight(w2_grouped, w2_raw[0])
+        round_weight(w2_grouped, w2_raw[1], on_vector=24)
         w2_q = quantise("w2", w2_grouped[:], H)
         x1_scales = pick("x1_scales", x_scale_tab, offs_l, U8)
         x1_words = pick("x1_words", x_word_tab, offs_l, U32)
@@ -152,9 +151,11 @@ def tile_picked_twqpullbprod_none_p_kernel(
         w1_q = quantise("w1", w1_grouped[:], H)
         picked_words = pick("picked_words", d_word_tab, k1_l, U32)
         code_words = sb("code_words", [P, H], U32)
-        deal(code_words, picked_words, GROUP)
+        dst, src = dealt_views(code_words, picked_words, RUN)
+        for t in range(PACK):
+            nc.sync.dma_start(dst[:, t], src[:, t])
         dealt_scales = keep.tile([P, H], U8, name="dealt_scales", tag="w1_raw256", align_bytes=64)
-        deal(dealt_scales, picked_scales, GROUP // 4)
+        nc.vector.tensor_copy(*dealt_views(dealt_scales, picked_scales, RUN // 4))
         for r in range(4):
             nc.sync.dma_start(code_scales[r:P:32, :].bitcast(I32), dealt_scales[8 * r : P : 32, :].bitcast(I32))
         differences(2)
@@ -219,7 +220,7 @@ def tile_picked_twqpullbprod_none_p_kernel(
             for c in range(len(Z_CHUNKS)):
                 coded_layer(c, t)
 
-        out_rows = out.rearrange("(g t q) n -> t g q n", t=PACK, q=GROUP)
+        out_rows = out.rearrange("(g t q) n -> t g q n", t=PACK, q=RUN)
         firsts = []
 
         def fetch(t):

from contextlib import ExitStack

import concourse.mybir as mybir

K, T, S, H, G = 512, 1024, 512, 512, 2048
FLOPS = 3 * 2 * K * H * S

F32 = mybir.dt.float32
BF16 = mybir.dt.bfloat16
I32 = mybir.dt.int32
U32 = mybir.dt.uint32
U16 = mybir.dt.uint16
U8 = mybir.dt.uint8
FP8X4 = mybir.dt.float8_e4m3fn_x4
ALU = mybir.AluOpType
ACT = mybir.ActivationFunctionType

P = 128
PACK = 4
GROUP = 16
RUN = 8
HALF = S // 2
Z_CHUNKS = ((0, 256), (256, 384), (384, 512))
LAST_PIECES = ((0, 256), (256, 384), (384, 512))


def tile_picked_twqpullbprod_none_p_kernel(
    tc, x_words, x_scales, w1, w2, gs, d_words, d_scales, offs, two, n1, n2, k1, n3, n4, out
):
    nc = tc.nc
    with ExitStack() as ctx:
        keep = ctx.enter_context(tc.tile_pool(name="keep", bufs=1))
        psum = ctx.enter_context(tc.psum_pool(name="psum", bufs=8))

        def sb(name, shape, dtype):
            return keep.tile(shape, dtype, name=name, align_bytes=64)

        def load_list(name, src):
            lst = keep.tile([P, S // GROUP], U16, name=name)
            nc.sync.dma_start(lst[:], src)
            return lst

        def entries(lst, lo, hi):
            return lst[:, lo // GROUP : hi // GROUP]

        x_scale_tab = sb("x_scale_tab", [P, T], U8)
        d_scale_tab = sb("d_scale_tab", [P, G], U8)
        code_scales = sb("code_scales", [P, H], U8)
        nc.gpsimd.memset(x_scale_tab[:].bitcast(I32), 0)
        windows = [sb(f"window{t}", [P, 2 * S], F32) for t in range(PACK)]
        nc.vector.memset(d_scale_tab[:].bitcast(I32), 0)
        for t in range(0, PACK, 2):
            nc.vector.memset(windows[t][:, S:], 0.0)
            nc.scalar.activation(windows[t + 1][:, S:], windows[t][:, S:], ACT.Sigmoid)
        nc.vector.memset(code_scales[:].bitcast(I32), 0)

        def load_weight(name, w, lo, hi):
            raw = sb(f"{name}_raw{lo}", [P, PACK, hi - lo], F32)
            nc.sync.dma_start(raw[:], w.rearrange("(p j) c -> p j c", j=PACK)[:, :, lo:hi])
            return raw, lo, hi

        two_l = load_list("two_l", two)
        k1_l = load_list("k1_l", k1)
        for q in range(4):
            nc.sync.dma_start(
                x_scale_tab[32 * q : 32 * q + 4, :].bitcast(I32), x_scales[0, 4 * q : 4 * q + 4, :].bitcast(I32)
            )
        nc.sync.dma_start(d_scale_tab[0:P:8, :].bitcast(I32), d_scales[0].bitcast(I32))
        w2_raw = [load_weight("w2", w2, 0, 256)]
        x_word_tab = sb("x_word_tab", [P, T], U32)
        nc.sync.dma_start(x_word_tab[:].bitcast(I32), x_words[0].rearrange("p n t -> p (n t)").bitcast(I32))
        w2_raw.append(load_weight("w2", w2, 256, 512))
        w1_raw = [load_weight("w1", w1, 0, 256)]
        offs_l = load_list("offs_l", offs)
        n2_l = load_list("n2_l", n2)
        w1_raw.append(load_weight("w1", w1, 256, 512))
        d_word_tab = sb("d_word_tab", [P, G], U32)
        nc.sync.dma_start(d_word_tab[:].bitcast(I32), d_words[0].rearrange("p n t -> p (n t)").bitcast(I32))
        gs_t = sb("gs_t", [P, PACK], F32)
        nc.sync.dma_start(gs_t[:], gs.rearrange("(p t) o -> p (t o)", t=PACK))
        n1_l = load_list("n1_l", n1)
        n3_l = load_list("n3_l", n3)
        n4_l = load_list("n4_l", n4)

        def pick(name, table, lst, dtype):
            picked = sb(name, [P, S], dtype)
            nc.vector.tensor_copy(picked[:], table[:].indirect(lst[:]))
            return picked

        x2_scales = pick("x2_scales", x_scale_tab, two_l, U8)
        picked_scales = pick("picked_scales", d_scale_tab, k1_l, U8)
        x2_words = pick("x2_words", x_word_tab, two_l, U32)

        def round_weight(grouped, piece, on_vector=0):
            raw, lo, hi = piece
            dst = grouped[:].rearrange("p (t m j) -> p m t j", t=PACK, j=PACK)[:, lo // PACK : hi // PACK, :, :]
            src = raw[:].rearrange("p j (m t) -> p m t j", t=PACK)
            if on_vector:
                nc.vector.tensor_copy(dst[:, :on_vector], src[:, :on_vector])
            nc.scalar.copy(dst[:, on_vector:], src[:, on_vector:])

        def dealt_views(dealt, picked, run):
            return (
                dealt[:].bitcast(I32).rearrange("p (t g r) -> p t g r", t=PACK, r=run),
                picked[:].bitcast(I32).rearrange("p (g t r) -> p t g r", t=PACK, r=run),
            )

        def quantise(name, grouped, width):
            codes = sb(f"{name}_codes", [P, width], U32)
            scales = sb(f"{name}_scales", [P, width], U8)
            nc.vector.quantize_mx(out=codes[:].bitcast(FP8X4), scales=scales[:], in_=grouped)
            return codes, scales

        def product(name, stat, t, moving, width):
            acc = psum.tile([P, width], F32, name=name, tag="bank")
            cols = slice(t * P, (t + 1) * P)
            nc.tensor.matmul_mx(
                out=acc[:],
                lhsT=stat[0][:, cols].bitcast(FP8X4),
                lhsT_scale=stat[1][:, cols],
                rhs=moving[0][:].bitcast(FP8X4),
                rhs_scale=moving[1][:],
                start=True,
                stop=True,
            )
            return acc

        w2_grouped = sb("w2_grouped", [P, PACK * H], BF16)
        w1_grouped = sb("w1_grouped", [P, PACK * H], BF16)
        round_weight(w2_grouped, w2_raw[0])
        round_weight(w2_grouped, w2_raw[1], on_vector=24)
        w2_q = quantise("w2", w2_grouped[:], H)
        x1_scales = pick("x1_scales", x_scale_tab, offs_l, U8)
        x1_words = pick("x1_words", x_word_tab, offs_l, U32)
        round_weight(w1_grouped, w1_raw[0])

        diffs = []

        def differences(t):
            acc = product(f"d_acc{t}", w2_q, t, (x2_words, x2_scales), S)
            own = sb(f"d_own{t}", [P, S], F32)
            nc.scalar.copy(windows[t][:, :S], acc[:])
            nc.scalar.copy(own[:], acc[:])
            diff = sb(f"diff{t}", [P, S], F32)
            nc.vector.tensor_tensor(diff[:], windows[t][:].indirect(n2_l[:]), own[:], ALU.subtract)
            diffs.append(diff)

        differences(0)
        differences(1)
        round_weight(w1_grouped, w1_raw[1])
        w1_q = quantise("w1", w1_grouped[:], H)
        picked_words = pick("picked_words", d_word_tab, k1_l, U32)
        code_words = sb("code_words", [P, H], U32)
        dst, src = dealt_views(code_words, picked_words, RUN)
        for t in range(PACK):
            nc.sync.dma_start(dst[:, t], src[:, t])
        dealt_scales = keep.tile([P, H], U8, name="dealt_scales", tag="w1_raw256", align_bytes=64)
        nc.vector.tensor_copy(*dealt_views(dealt_scales, picked_scales, RUN // 4))
        for r in range(4):
            nc.sync.dma_start(code_scales[r:P:32, :].bitcast(I32), dealt_scales[8 * r : P : 32, :].bitcast(I32))
        differences(2)
        differences(3)

        y_own = sb("y_own", [P, PACK, S], F32)
        step = sb("step", [P, PACK, S], F32)
        pulls, gates = [], []

        def make_gate(t):
            gate = sb(f"gate{t}", [P, S], F32)
            nc.scalar.activation(gate[:], diffs[t][:], ACT.Sigmoid)
            gates.append(gate)

        def gated(t, lo, hi):
            nc.vector.tensor_tensor(step[:, t, lo:hi], gates[t][:, lo:hi], pulls[t][:, lo:hi], ALU.mult)

        for t in range(PACK):
            acc = product(f"y_acc{t}", w1_q, t, (x1_words, x1_scales), S)
            nc.scalar.activation(windows[t][:, :S], acc[:], ACT.Copy, scale=gs_t[:, t : t + 1])
            nc.scalar.activation(y_own[:, t, :], acc[:], ACT.Copy, scale=gs_t[:, t : t + 1])
            pull = sb(f"pull{t}", [P, S], F32)
            nc.vector.tensor_tensor(pull[:], windows[t][:].indirect(n1_l[:]), y_own[:, t, :], ALU.subtract)
            pulls.append(pull)
            if t > 0:
                make_gate(t - 1)
                gated(t - 1, 0, S)
        make_gate(PACK - 1)
        gated(PACK - 1, 0, HALF)
        gated(PACK - 1, HALF, S)

        z_grouped = []

        def blend(c):
            lo, hi = Z_CHUNKS[c]
            grouped = sb(f"z_grouped{c}", [P, PACK * (hi - lo)], BF16)
            nc.vector.tensor_tensor(
                grouped[:].rearrange("p (c i t) -> p c t i", t=PACK, i=4),
                step[:, :, lo:hi].rearrange("p t (c i) -> p c t i", i=4),
                y_own[:, :, lo:hi].rearrange("p t (c i) -> p c t i", i=4),
                ALU.add,
            )
            z_grouped.append(grouped)

        z_q = []

        def quantise_z(c):
            lo, hi = Z_CHUNKS[c]
            z_q.append(quantise(f"z{c}", z_grouped[c][:], hi - lo))

        def coded_layer(c, t):
            lo, hi = Z_CHUNKS[c]
            acc = product(f"h_acc{c}_{t}", (code_words, code_scales), t, z_q[c], hi - lo)
            nc.scalar.activation(windows[t][:, lo:hi], acc[:], ACT.Copy, scale=0.0625)

        blend(0)
        for c in range(1, len(Z_CHUNKS)):
            blend(c)
            quantise_z(c - 1)
        quantise_z(len(Z_CHUNKS) - 1)
        for t in range(PACK):
            for c in range(len(Z_CHUNKS)):
                coded_layer(c, t)

        out_rows = out.rearrange("(g t q) n -> t g q n", t=PACK, q=RUN)
        firsts = []

        def fetch(t):
            first = sb(f"first{t}", [P, S], F32)
            nc.vector.tensor_copy(first[:], windows[t][:].indirect(n3_l[:]))
            firsts.append(first)

        def finish(t, pieces):
            res = sb(f"res{t}", [P, S], F32)
            for lo, hi in pieces:
                nc.vector.tensor_tensor(res[:, lo:hi], windows[t][:].indirect(entries(n4_l, lo, hi)), firsts[t][:, lo:hi], ALU.mult)
                nc.sync.dma_start(out_rows[t][:, :, lo:hi], res[:, lo:hi])

        fetch(0)
        for t in range(1, PACK):
            fetch(t)
            finish(t - 1, ((0, S),))
        finish(PACK - 1, LAST_PIECES)
